import numpy as np
import ml_dtypes


def mxq(x, axis, fmt="e4m3"):
    dtype, down = {"e4m3": (ml_dtypes.float8_e4m3fn, 7), "e5m2": (ml_dtypes.float8_e5m2, 14)}[fmt]
    v = np.moveaxis(np.asarray(x, np.float32).astype(ml_dtypes.bfloat16).astype(np.float64), axis, -1)
    blocks = v.reshape(v.shape[:-1] + (-1, 32))
    amax = np.abs(blocks).max(-1, keepdims=True)
    byte = np.maximum(np.where(amax > 0, np.frexp(amax)[1] - 1 + 127, 0) - down, 1)
    scale = np.exp2(byte - 127.0)
    codes = (blocks / scale).astype(np.float32).astype(dtype).astype(np.float64)
    return np.moveaxis((codes * scale).reshape(v.shape), -1, axis)


WIDE = False


def mx_kscale(k):
    if not WIDE:
        return np.ones(k)
    levels = np.array([10, -10, 5, -5, 0])
    if k % 512:
        return np.exp2(np.random.permutation(np.resize(levels, k // 32))).repeat(32)
    a = np.empty((k // 512, 16))
    for p in range(k // 512):
        a[p, :8] = np.random.permutation(np.resize(levels, 8))
        for g in range(8):
            far = levels[np.abs(levels - a[p, g]) >= 10]
            a[p, g + 8] = far[np.random.randint(len(far))]
    return np.exp2(a.ravel()).repeat(32)


def f64(x):
    return np.asarray(x).astype(np.float64)


def striped(idx):
    return np.tile(idx.reshape(-1, 16).T, (8, 1)).astype(np.uint16)


def unstriped(offs):
    return offs[:16].T.reshape(-1).astype(np.int64)


def striped8(idx):
    return np.concatenate([x.reshape(-1, 16).T for x in idx]).astype(np.uint16)


def runs(offs, k):
    lists = np.stack([offs[16 * r : 16 * r + 16].T.reshape(-1) for r in range(8)]).astype(np.int64)
    return lists[np.arange(k) % 512 // 64]


def pack_weight(w):
    k, n = w.shape
    w = f64(np.asarray(w, np.float32).astype(ml_dtypes.bfloat16)).reshape(k // 32, 32, n)
    amax = np.abs(w).max(1)
    byte = np.clip(np.where(amax > 0, np.frexp(amax)[1] - 1 + 127 - 7, 1), 1, 254)
    scaled = (w * np.exp2(127.0 - byte)[:, None, :]).reshape(k, n).astype(np.float32)
    words = np.ascontiguousarray(scaled.reshape(k // 512, 128, 4, n).transpose(0, 1, 3, 2)).astype(ml_dtypes.float8_e4m3fn).view(np.uint8)
    return words, np.ascontiguousarray(byte.astype(np.uint8).reshape(k // 512, 16, n))


def unpack_weight(words, scales):
    g, p, n, _ = words.shape
    vals = np.ascontiguousarray(words).view(ml_dtypes.float8_e4m3fn).astype(np.float64) * np.repeat(np.exp2(scales.astype(np.float64) - 127.0), 8, axis=1)[..., None]
    return vals.transpose(0, 1, 3, 2).reshape(g * 512, n)


def sigmoid(v):
    return 1.0 / (1.0 + np.exp(-np.maximum(v, -700.0)))

def planes(y):
    n, m = y.shape
    v = y.astype(np.float32).astype(ml_dtypes.bfloat16).astype(np.float64).reshape(n // 32, 32, m)
    top = np.abs(v).max(1)
    byte = np.clip(np.where(top > 0, np.frexp(top)[1] - 1 + 127 - 7, 1), 1, 254)
    codes = (v * np.exp2(127.0 - byte)[:, None, :]).reshape(n, m).astype(np.float32).astype(ml_dtypes.float8_e4m3fn).view(np.uint8)
    words = codes.reshape(n // 512, 128, 4, m).transpose(0, 1, 3, 2)
    return np.ascontiguousarray(words), np.ascontiguousarray(byte.astype(np.uint8).reshape(n // 512, 16, m))


K, T, S, N, H = 512, 2048, 512, 512, 512


def setup_inputs():
    n = np.random.standard_normal
    s = mx_kscale(K)[:, None]
    u = mx_kscale(S)
    packed_xT = pack_weight(n((K, T)) * s)
    return {
        "x_words": packed_xT[0],
        "x_scales": packed_xT[1],
        "wa": (n((K, H)) / np.sqrt(K) / s).astype(np.float32),
        "wb": (n((K, N)) / np.sqrt(K) / s).astype(np.float32),
        "gt": (np.random.uniform(0.5, 1.5, (S, 1)) * u[:, None]).astype(np.float32),
        "gi": (np.random.uniform(0.5, 1.5, (S, 1)) / u[:, None]).astype(np.float32),
        "offs": striped(np.random.permutation(T)[:S]),
        "two": striped(np.random.permutation(T)[:S]),
        "n1": striped(np.random.permutation(H)),
        "n2": striped(np.random.permutation(H)),
        "n3": striped8(np.stack([np.random.permutation(N) for _ in range(8)])),
        "n4": striped8(np.stack([np.random.permutation(N) for _ in range(8)])),
        "n5": striped8(np.stack([np.random.permutation(N) for _ in range(8)])),
    }


def reference(x_words, x_scales, wa, wb, gt, gi, offs, two, n1, n2, n3, n4, n5):
    xq = unpack_weight(x_words, x_scales)[:, unstriped(offs)]
    a = xq.T @ mxq(f64(wa), 0, "e4m3")
    z = f64(gt) * (a + (sigmoid(a[:, unstriped(n1)])) * (a[:, unstriped(n2)] - a))
    x_two = unpack_weight(x_words, x_scales)[:, unstriped(two)]
    b = x_two.T @ mxq(f64(wb), 0, "e4m3")
    z2 = f64(gi) * b
    cv = 0.0625 * ((mxq(z, 0, "e4m3").T @ mxq(z2, 0, "e4m3")))
    out_0 = cv + cv[np.arange(H)[:, None], runs(n3, H)] - (np.maximum(cv[np.arange(H)[:, None], runs(n4, H)], cv[np.arange(H)[:, None], runs(n5, H)]))
    return (out_0,) + planes(out_0)

@@ -1,0 +1,194 @@
+from contextlib import ExitStack
+
+import concourse.mybir as mybir
+
+F32 = mybir.dt.float32
+BF16 = mybir.dt.bfloat16
+I32 = mybir.dt.int32
+U32 = mybir.dt.uint32
+U16 = mybir.dt.uint16
+U8 = mybir.dt.uint8
+FP8X4 = mybir.dt.float8_e4m3fn_x4
+ALU = mybir.AluOpType
+ACT = mybir.ActivationFunctionType
+
+P = 128
+PACK = 4
+T = 2048
+W = 512
+HALF = 256
+HL = HALF // 16
+FLOPS = 3 * 2 * 512 * 512 * 512
+
+
+def tile_picked_momtracktrim_none_po_kernel(
+    tc, x_words, x_scales, wa, wb, gt, gi, offs, two, n1, n2, n3, n4, n5, out_0, out_1, out_2
+):
+    nc = tc.nc
+    with ExitStack() as ctx:
+        keep = ctx.enter_context(tc.tile_pool(name="keep", bufs=1))
+        psum = ctx.enter_context(tc.psum_pool(name="psum", bufs=1))
+
+        def sb(name, shape, dtype):
+            return keep.tile(shape, dtype, name=name, align_bytes=64)
+
+        def load_list(name, src):
+            tile = keep.tile([P, W // 16], U16, name=name)
+            nc.sync.dma_start(tile[:], src)
+            return tile
+
+        def half_of(lst, h):
+            return lst[:, h * HL : (h + 1) * HL]
+
+        def cols(h):
+            return slice(h * HALF, (h + 1) * HALF)
+
+        xs = sb("xs", [P, T], U8)
+        nc.vector.memset(xs[:].bitcast(I32), 0)
+        l_offs = load_list("l_offs", offs)
+        for q in range(4):
+            nc.sync.dma_start(xs[32 * q : 32 * q + 4, :].bitcast(I32), x_scales[0, 4 * q : 4 * q + 4, :].bitcast(I32))
+        l_two = load_list("l_two", two)
+        xw = sb("xw", [P, T], U32)
+        nc.sync.dma_start(xw[:].bitcast(I32), x_words[0].rearrange("p n t -> p (n t)").bitcast(I32))
+        raw = {}
+        for name, w in (("wa", wa), ("wb", wb)):
+            for h in range(2):
+                raw[name, h] = sb("raw_%s%d" % (name, h), [P, PACK, HALF], F32)
+                nc.sync.dma_start(raw[name, h][:], w.rearrange("(p j) c -> p j c", j=PACK)[:, :, cols(h)])
+            if name == "wa":
+                l_n1 = load_list("l_n1", n1)
+                l_n2 = load_list("l_n2", n2)
+        gt_sb = sb("gt_sb", [P, PACK], F32)
+        gi_sb = sb("gi_sb", [P, PACK], F32)
+        nc.gpsimd.dma_start(gt_sb[:], gt.rearrange("(p t) o -> p (t o)", t=PACK))
+        nc.gpsimd.dma_start(gi_sb[:], gi.rearrange("(p t) o -> p (t o)", t=PACK))
+        l_n5 = load_list("l_n5", n5)
+        l_n4 = load_list("l_n4", n4)
+        l_n3 = load_list("l_n3", n3)
+
+        def dealt(tile):
+            return tile[:].rearrange("p (t m) -> p m t", t=PACK)
+
+        pick_s = {}
+        pick_w = {}
+        for name, lst in (("wa", l_offs), ("wb", l_two)):
+            pick_s[name] = sb("pick_s_" + name, [P, W], U8)
+            nc.vector.tensor_copy(dealt(pick_s[name]), xs[:].indirect(lst[:]))
+        for name, lst in (("wa", l_offs), ("wb", l_two)):
+            pick_w[name] = sb("pick_w_" + name, [P, W], U32)
+            nc.vector.tensor_copy(dealt(pick_w[name]), xw[:].indirect(lst[:]))
+
+        def interleave(copy, dst, src):
+            copy(
+                dst.rearrange("p (c i t) -> p c t i", i=4, t=PACK),
+                src.rearrange("p t (c i) -> p c t i", i=4),
+            )
+
+        w_codes = {}
+        w_scales = {}
+
+        def weights(name, engines):
+            w_codes[name] = sb("codes_" + name, [P, W], U32)
+            w_scales[name] = sb("scales_" + name, [P, W], U8)
+            rounded = []
+            for h in range(2):
+                r = sb("round_%s%d" % (name, h), [P, PACK * HALF], BF16)
+                interleave(engines[h], r[:], raw[name, h][:])
+                rounded.append(r)
+            for h in range(2):
+                nc.vector.quantize_mx(w_codes[name][:, cols(h)].bitcast(FP8X4), w_scales[name][:, cols(h)], rounded[h][:])
+
+        def product(bank, lc, ls, t, rc, rs):
+            m = slice(t * P, (t + 1) * P)
+            nc.tensor.matmul_mx(
+                bank[:], lhsT=lc[:, m].bitcast(FP8X4), lhsT_scale=ls[:, m], rhs=rc[:].bitcast(FP8X4), rhs_scale=rs[:],
+                start=True, stop=True,
+            )
+
+        weights("wa", (nc.scalar.copy, nc.vector.tensor_copy))
+        a_ps = [psum.tile([P, W], F32, name="a_ps%d" % t, tag="bank%d" % t) for t in range(PACK)]
+        for t in range(PACK):
+            product(a_ps[t], pick_w["wa"], pick_s["wa"], t, w_codes["wa"], w_scales["wa"])
+        weights("wb", (nc.vector.tensor_copy, nc.vector.tensor_copy))
+        b_ps = [psum.tile([P, W], F32, name="b_ps%d" % t, tag="bank%d" % (4 + t)) for t in range(PACK)]
+        for t in range(PACK):
+            product(b_ps[t], pick_w["wb"], pick_s["wb"], t, w_codes["wb"], w_scales["wb"])
+
+        a_sb = [sb("a_sb%d" % t, [P, W], F32) for t in range(PACK)]
+        zb = sb("zb", [P, PACK * W], BF16)
+        zb_view = zb[:].rearrange("p (k m t) -> p m t k", k=PACK, t=PACK)
+        z2p = sb("z2p", [P, PACK, W], BF16)
+        for h in range(2):
+            s = sb("s%d" % h, [P, PACK, HALF], F32)
+            sg = sb("sg%d" % h, [P, PACK, HALF], F32)
+            v = sb("v%d" % h, [P, PACK, HALF], F32)
+            u = sb("u%d" % h, [P, PACK, HALF], F32)
+            for t in range(PACK + 1):
+                if t < PACK:
+                    if h == 0:
+                        nc.scalar.copy(a_sb[t][:], a_ps[t][:])
+                    nc.scalar.activation(s[:, t, :], a_sb[t][:].indirect(half_of(l_n1, h)), ACT.Sigmoid)
+                    nc.vector.tensor_scalar(sg[:, t, :], s[:, t, :], gt_sb[:, t : t + 1], None, ALU.mult)
+                if t > 0:
+                    nc.vector.scalar_tensor_tensor(
+                        u[:, t - 1, :], sg[:, t - 1, :], gt_sb[:, t - 1 : t], a_sb[t - 1][:, cols(h)], ALU.subtract, ALU.mult
+                    )
+                if t < PACK:
+                    nc.vector.tensor_tensor(v[:, t, :], a_sb[t][:].indirect(half_of(l_n2, h)), sg[:, t, :], ALU.mult)
+            nc.vector.tensor_tensor(
+                zb_view[:, h * 64 : (h + 1) * 64, :, :],
+                v[:].rearrange("p t (m k) -> p m t k", k=PACK),
+                u[:].rearrange("p t (m k) -> p m t k", k=PACK),
+                ALU.subtract,
+            )
+        for t in range(PACK):
+            nc.scalar.activation(z2p[:, t, :], b_ps[t][:], ACT.Copy, scale=gi_sb[:, t : t + 1])
+        z2b = sb("z2b", [P, PACK * W], BF16)
+        interleave(nc.scalar.copy, z2b[:], z2p[:])
+        z2_codes = sb("z2_codes", [P, W], U32)
+        z2_scales = sb("z2_scales", [P, W], U8)
+        nc.vector.quantize_mx(z2_codes[:].bitcast(FP8X4), z2_scales[:], z2b[:])
+        z_codes = sb("z_codes", [P, W], U32)
+        z_scales = sb("z_scales", [P, W], U8)
+        cv_ps = [psum.tile([P, W], F32, name="cv_ps%d" % k, tag="bank%d" % k) for k in range(PACK)]
+        for k in range(PACK):
+            m = slice(k * P, (k + 1) * P)
+            nc.vector.quantize_mx(z_codes[:, m].bitcast(FP8X4), z_scales[:, m], zb[:, k * W : (k + 1) * W])
+            product(cv_ps[k], z_codes, z_scales, k, z2_codes, z2_scales)
+
+        cv = [sb("cv%d" % k, [P, W], F32) for k in range(PACK)]
+        y_codes = sb("y_codes", [P, W], U32)
+        y_scales = sb("y_scales", [P, W], U8)
+        out_rows = out_0.rearrange("(p k) n -> p k n", k=PACK)
+        out_words = out_1[0].rearrange("p n t -> p (n t)").bitcast(I32)
+        for h in range(2):
+            g3 = sb("g3_%d" % h, [P, PACK, HALF], F32)
+            g4 = sb("g4_%d" % h, [P, PACK, HALF], F32)
+            g5 = sb("g5_%d" % h, [P, PACK, HALF], F32)
+            top = sb("top%d" % h, [P, PACK, HALF], F32)
+            r = sb("r%d" % h, [P, PACK, HALF], F32)
+            y = sb("y%d" % h, [P, PACK, HALF], F32)
+            for k in range(PACK + 1):
+                if k < PACK:
+                    if h == 0:
+                        if k == 1:
+                            nc.vector.tensor_scalar(cv[k][:], cv_ps[k][:], 0.0625, None, ALU.mult)
+                        else:
+                            nc.scalar.activation(cv[k][:], cv_ps[k][:], ACT.Copy, scale=0.0625)
+                    nc.scalar.activation(g5[:, k, :], cv[k][:].indirect(half_of(l_n5, h)), ACT.Copy)
+                    nc.scalar.activation(g3[:, k, :], cv[k][:].indirect(half_of(l_n3, h)), ACT.Copy)
+                    nc.vector.tensor_copy(g4[:, k, :], cv[k][:].indirect(half_of(l_n4, h)))
+                if k > 0:
+                    j = k - 1
+                    nc.vector.tensor_tensor(top[:, j, :], g4[:, j, :], g5[:, j, :], ALU.max)
+                    nc.vector.tensor_tensor(r[:, j, :], cv[j][:, cols(h)], g3[:, j, :], ALU.add)
+                    nc.vector.tensor_tensor(y[:, j, :], r[:, j, :], top[:, j, :], ALU.subtract)
+                    nc.sync.dma_start(out_rows[:, j, cols(h)], y[:, j, :])
+            yb = sb("yb%d" % h, [P, PACK * HALF], BF16)
+            interleave(nc.vector.tensor_copy, yb[:], y[:])
+            nc.vector.quantize_mx(y_codes[:, cols(h)].bitcast(FP8X4), y_scales[:, cols(h)], yb[:])
+            nc.sync.dma_start(out_words[:, cols(h)], y_codes[:, cols(h)].bitcast(I32))
+        for q in range(4):
+            queue = nc.scalar if q % 2 == 0 else nc.sync
+            queue.dma_start(out_2[0, 4 * q : 4 * q + 4, :].bitcast(I32), y_scales[32 * q : 32 * q + 4, :].bitcast(I32))

@@ -19,6 +19,12 @@ W = 512
 HALF = 256
 HL = HALF // 16
 FLOPS = 3 * 2 * 512 * 512 * 512
+GA_ON_SCALAR = ()
+SG_ON_POOL = False
+Z2_ON_SCALAR = True
+N4_ON_SCALAR = ()
+Y_ON_POOL = (0, 1, 2)
+WARM = False
 
 
 def tile_picked_momtracktrim_none_po_kernel(
@@ -29,8 +35,8 @@ def tile_picked_momtracktrim_none_po_kernel(
         keep = ctx.enter_context(tc.tile_pool(name="keep", bufs=1))
         psum = ctx.enter_context(tc.psum_pool(name="psum", bufs=1))
 
-        def sb(name, shape, dtype):
-            return keep.tile(shape, dtype, name=name, align_bytes=64)
+        def sb(name, shape, dtype, tag=None):
+            return keep.tile(shape, dtype, name=name, tag=tag or name, align_bytes=64)
 
         def load_list(name, src):
             tile = keep.tile([P, W // 16], U16, name=name)
@@ -44,39 +50,58 @@ def tile_picked_momtracktrim_none_po_kernel(
             return slice(h * HALF, (h + 1) * HALF)
 
         xs = sb("xs", [P, T], U8)
-        nc.vector.memset(xs[:].bitcast(I32), 0)
-        l_offs = load_list("l_offs", offs)
+        nc.vector.memset(xs[:, :1664].bitcast(I32), 0)
+        nc.gpsimd.memset(xs[:, 1664:].bitcast(I32), 0)
+        if WARM:
+            warm_in = sb("warm_in", [P, 1], F32)
+            warm_out = sb("warm_out", [P, 1], F32)
+            nc.gpsimd.memset(warm_in[:], 0.0)
+            nc.scalar.activation(warm_out[:], warm_in[:], ACT.Sigmoid)
         for q in range(4):
             nc.sync.dma_start(xs[32 * q : 32 * q + 4, :].bitcast(I32), x_scales[0, 4 * q : 4 * q + 4, :].bitcast(I32))
+        raw = {}
+
+        def load_weights(name, w, h):
+            raw[name, h] = sb("raw_%s%d" % (name, h), [P, PACK, HALF], F32)
+            nc.sync.dma_start(raw[name, h][:], w.rearrange("(p j) c -> p j c", j=PACK)[:, :, cols(h)])
+
+        l_offs = load_list("l_offs", offs)
+        load_weights("wa", wa, 0)
         l_two = load_list("l_two", two)
+        load_weights("wa", wa, 1)
         xw = sb("xw", [P, T], U32)
         nc.sync.dma_start(xw[:].bitcast(I32), x_words[0].rearrange("p n t -> p (n t)").bitcast(I32))
-        raw = {}
-        for name, w in (("wa", wa), ("wb", wb)):
-            for h in range(2):
-                raw[name, h] = sb("raw_%s%d" % (name, h), [P, PACK, HALF], F32)
-                nc.sync.dma_start(raw[name, h][:], w.rearrange("(p j) c -> p j c", j=PACK)[:, :, cols(h)])
-            if name == "wa":
-                l_n1 = load_list("l_n1", n1)
-                l_n2 = load_list("l_n2", n2)
+        l_n1 = load_list("l_n1", n1)
+        load_weights("wb", wb, 0)
+        load_weights("wb", wb, 1)
         gt_sb = sb("gt_sb", [P, PACK], F32)
         gi_sb = sb("gi_sb", [P, PACK], F32)
-        nc.gpsimd.dma_start(gt_sb[:], gt.rearrange("(p t) o -> p (t o)", t=PACK))
-        nc.gpsimd.dma_start(gi_sb[:], gi.rearrange("(p t) o -> p (t o)", t=PACK))
+        nc.sync.dma_start(gt_sb[:], gt.rearrange("(p t) o -> p (t o)", t=PACK))
+        l_n2 = load_list("l_n2", n2)
+        nc.sync.dma_start(gi_sb[:], gi.rearrange("(p t) o -> p (t o)", t=PACK))
+        l_n3 = load_list("l_n3", n3)
         l_n5 = load_list("l_n5", n5)
         l_n4 = load_list("l_n4", n4)
-        l_n3 = load_list("l_n3", n3)
+
+        a_sb = [sb("a_sb%d" % t, [P, 2 * W], F32) for t in range(PACK)]
+        ga_sb = {t: sb("ga_sb%d" % t, [P, 2 * W], F32) for t in GA_ON_SCALAR}
+        for t in range(PACK):
+            nc.gpsimd.memset(a_sb[t][:, W:], 0.0)
+        for t in GA_ON_SCALAR:
+            nc.gpsimd.memset(ga_sb[t][:, W:], 0.0)
 
         def dealt(tile):
             return tile[:].rearrange("p (t m) -> p m t", t=PACK)
 
         pick_s = {}
         pick_w = {}
-        for name, lst in (("wa", l_offs), ("wb", l_two)):
+
+        def pick_scales(name, lst):
             pick_s[name] = sb("pick_s_" + name, [P, W], U8)
             nc.vector.tensor_copy(dealt(pick_s[name]), xs[:].indirect(lst[:]))
-        for name, lst in (("wa", l_offs), ("wb", l_two)):
-            pick_w[name] = sb("pick_w_" + name, [P, W], U32)
+
+        def pick_words(name, lst, tag=None):
+            pick_w[name] = sb("pick_w_" + name, [P, W], U32, tag)
             nc.vector.tensor_copy(dealt(pick_w[name]), xw[:].indirect(lst[:]))
 
         def interleave(copy, dst, src):
@@ -89,13 +114,16 @@ def tile_picked_momtracktrim_none_po_kernel(
         w_scales = {}
 
         def weights(name, engines):
-            w_codes[name] = sb("codes_" + name, [P, W], U32)
-            w_scales[name] = sb("scales_" + name, [P, W], U8)
             rounded = []
             for h in range(2):
                 r = sb("round_%s%d" % (name, h), [P, PACK * HALF], BF16)
                 interleave(engines[h], r[:], raw[name, h][:])
                 rounded.append(r)
+            return rounded
+
+        def quantise_weights(name, rounded):
+            w_codes[name] = sb("codes_" + name, [P, W], U32)
+            w_scales[name] = sb("scales_" + name, [P, W], U8, "xs" if name == "wa" else None)
             for h in range(2):
                 nc.vector.quantize_mx(w_codes[name][:, cols(h)].bitcast(FP8X4), w_scales[name][:, cols(h)], rounded[h][:])
 
@@ -106,89 +134,118 @@ def tile_picked_momtracktrim_none_po_kernel(
                 start=True, stop=True,
             )
 
-        weights("wa", (nc.scalar.copy, nc.vector.tensor_copy))
+        pick_scales("wa", l_offs)
+        pick_scales("wb", l_two)
+        quantise_weights("wa", weights("wa", (nc.scalar.copy, nc.scalar.copy)))
+        pick_words("wa", l_offs)
         a_ps = [psum.tile([P, W], F32, name="a_ps%d" % t, tag="bank%d" % t) for t in range(PACK)]
         for t in range(PACK):
             product(a_ps[t], pick_w["wa"], pick_s["wa"], t, w_codes["wa"], w_scales["wa"])
-        weights("wb", (nc.vector.tensor_copy, nc.vector.tensor_copy))
-        b_ps = [psum.tile([P, W], F32, name="b_ps%d" % t, tag="bank%d" % (4 + t)) for t in range(PACK)]
-        for t in range(PACK):
-            product(b_ps[t], pick_w["wb"], pick_s["wb"], t, w_codes["wb"], w_scales["wb"])
+        pick_words("wb", l_two)
+        quantise_weights("wb", weights("wb", (nc.vector.tensor_copy, nc.vector.tensor_copy)))
+        b_ps = [psum.tile([P, W], F32, name="b_ps%d" % j, tag="bank%d" % (4 + j)) for j in range(PACK)]
+        for j in range(PACK):
+            product(b_ps[j], pick_w["wb"], pick_s["wb"], j, w_codes["wb"], w_scales["wb"])
 
-        a_sb = [sb("a_sb%d" % t, [P, W], F32) for t in range(PACK)]
         zb = sb("zb", [P, PACK * W], BF16)
-        zb_view = zb[:].rearrange("p (k m t) -> p m t k", k=PACK, t=PACK)
         z2p = sb("z2p", [P, PACK, W], BF16)
-        for h in range(2):
-            s = sb("s%d" % h, [P, PACK, HALF], F32)
-            sg = sb("sg%d" % h, [P, PACK, HALF], F32)
-            v = sb("v%d" % h, [P, PACK, HALF], F32)
-            u = sb("u%d" % h, [P, PACK, HALF], F32)
-            for t in range(PACK + 1):
-                if t < PACK:
-                    if h == 0:
-                        nc.scalar.copy(a_sb[t][:], a_ps[t][:])
-                    nc.scalar.activation(s[:, t, :], a_sb[t][:].indirect(half_of(l_n1, h)), ACT.Sigmoid)
-                    nc.vector.tensor_scalar(sg[:, t, :], s[:, t, :], gt_sb[:, t : t + 1], None, ALU.mult)
-                if t > 0:
-                    nc.vector.scalar_tensor_tensor(
-                        u[:, t - 1, :], sg[:, t - 1, :], gt_sb[:, t - 1 : t], a_sb[t - 1][:, cols(h)], ALU.subtract, ALU.mult
-                    )
-                if t < PACK:
-                    nc.vector.tensor_tensor(v[:, t, :], a_sb[t][:].indirect(half_of(l_n2, h)), sg[:, t, :], ALU.mult)
-            nc.vector.tensor_tensor(
-                zb_view[:, h * 64 : (h + 1) * 64, :, :],
-                v[:].rearrange("p t (m k) -> p m t k", k=PACK),
-                u[:].rearrange("p t (m k) -> p m t k", k=PACK),
-                ALU.subtract,
+        s = sb("s", [P, PACK, W], F32)
+        sg = sb("sg", [P, PACK, W], F32, "round_wb1")
+        v = sb("v", [P, PACK, W], F32)
+        u = sb("u", [P, PACK, W], F32)
+
+        def gate(t):
+            gt_col = gt_sb[:, t : t + 1]
+            nc.scalar.copy(a_sb[t][:, :W], a_ps[t][:])
+            nc.scalar.activation(s[:, t, :], a_sb[t][:].indirect(l_n1[:]), ACT.Sigmoid)
+            if t in ():
+                nc.gpsimd.tensor_scalar(sg[:, t, :], s[:, t, :], gt_col, 0.0, ALU.mult, ALU.add)
+            elif t in (3,):
+                nc.scalar.activation(sg[:, t, :], s[:, t, :], ACT.Copy, scale=gt_col)
+            else:
+                nc.vector.tensor_scalar(sg[:, t, :], s[:, t, :], gt_col, None, ALU.mult)
+
+        gate(0)
+        for t in range(PACK):
+            nc.vector.tensor_tensor(v[:, t, :], a_sb[t][:].indirect(l_n2[:]), sg[:, t, :], ALU.mult)
+            if t + 1 < PACK:
+                gate(t + 1)
+            nc.vector.scalar_tensor_tensor(
+                u[:, t, :], sg[:, t, :], gt_sb[:, t : t + 1], a_ps[t][:], ALU.subtract, ALU.mult
             )
         for t in range(PACK):
             nc.scalar.activation(z2p[:, t, :], b_ps[t][:], ACT.Copy, scale=gi_sb[:, t : t + 1])
         z2b = sb("z2b", [P, PACK * W], BF16)
-        interleave(nc.scalar.copy, z2b[:], z2p[:])
-        z2_codes = sb("z2_codes", [P, W], U32)
         z2_scales = sb("z2_scales", [P, W], U8)
-        nc.vector.quantize_mx(z2_codes[:].bitcast(FP8X4), z2_scales[:], z2b[:])
+        if Z2_ON_SCALAR:
+            interleave(nc.scalar.copy, z2b[:], z2p[:])
+        nc.vector.tensor_tensor(
+            zb[:].rearrange("p (k m t) -> p m t k", k=PACK, t=PACK),
+            v[:].rearrange("p t (m k) -> p m t k", k=PACK),
+            u[:].rearrange("p t (m k) -> p m t k", k=PACK),
+            ALU.subtract,
+        )
+        if not Z2_ON_SCALAR:
+            interleave(nc.vector.tensor_copy, z2b[:], z2p[:])
         z_codes = sb("z_codes", [P, W], U32)
         z_scales = sb("z_scales", [P, W], U8)
         cv_ps = [psum.tile([P, W], F32, name="cv_ps%d" % k, tag="bank%d" % k) for k in range(PACK)]
+        z2_codes = sb("z2_codes", [P, W], U32, "v")
+        nc.vector.quantize_mx(z2_codes[:].bitcast(FP8X4), z2_scales[:], z2b[:])
         for k in range(PACK):
             m = slice(k * P, (k + 1) * P)
             nc.vector.quantize_mx(z_codes[:, m].bitcast(FP8X4), z_scales[:, m], zb[:, k * W : (k + 1) * W])
             product(cv_ps[k], z_codes, z_scales, k, z2_codes, z2_scales)
 
-        cv = [sb("cv%d" % k, [P, W], F32) for k in range(PACK)]
+        cv = a_sb
         y_codes = sb("y_codes", [P, W], U32)
         y_scales = sb("y_scales", [P, W], U8)
         out_rows = out_0.rearrange("(p k) n -> p k n", k=PACK)
         out_words = out_1[0].rearrange("p n t -> p (n t)").bitcast(I32)
-        for h in range(2):
-            g3 = sb("g3_%d" % h, [P, PACK, HALF], F32)
-            g4 = sb("g4_%d" % h, [P, PACK, HALF], F32)
-            g5 = sb("g5_%d" % h, [P, PACK, HALF], F32)
-            top = sb("top%d" % h, [P, PACK, HALF], F32)
-            r = sb("r%d" % h, [P, PACK, HALF], F32)
-            y = sb("y%d" % h, [P, PACK, HALF], F32)
-            for k in range(PACK + 1):
-                if k < PACK:
-                    if h == 0:
-                        if k == 1:
-                            nc.vector.tensor_scalar(cv[k][:], cv_ps[k][:], 0.0625, None, ALU.mult)
-                        else:
-                            nc.scalar.activation(cv[k][:], cv_ps[k][:], ACT.Copy, scale=0.0625)
-                    nc.scalar.activation(g5[:, k, :], cv[k][:].indirect(half_of(l_n5, h)), ACT.Copy)
-                    nc.scalar.activation(g3[:, k, :], cv[k][:].indirect(half_of(l_n3, h)), ACT.Copy)
-                    nc.vector.tensor_copy(g4[:, k, :], cv[k][:].indirect(half_of(l_n4, h)))
-                if k > 0:
-                    j = k - 1
-                    nc.vector.tensor_tensor(top[:, j, :], g4[:, j, :], g5[:, j, :], ALU.max)
-                    nc.vector.tensor_tensor(r[:, j, :], cv[j][:, cols(h)], g3[:, j, :], ALU.add)
-                    nc.vector.tensor_tensor(y[:, j, :], r[:, j, :], top[:, j, :], ALU.subtract)
-                    nc.sync.dma_start(out_rows[:, j, cols(h)], y[:, j, :])
+        g3 = sb("g3", [P, PACK, W], F32)
+        g4 = sb("g4", [P, PACK, W], F32)
+        g5 = sb("g5", [P, PACK, W], F32)
+        top = sb("top", [P, PACK, W], F32)
+        r = sb("r", [P, PACK, W], F32)
+        y = sb("y", [P, PACK, W], F32)
+        steps = [(0, 0, W), (1, 0, W), (2, 0, W), (3, 0, HALF), (3, HALF, W)]
+
+        def fetch(i):
+            k, c0, c1 = steps[i]
+            if c0 == 0:
+                if k in (1, 2):
+                    nc.vector.tensor_scalar(cv[k][:, :W], cv_ps[k][:], 0.0625, None, ALU.mult)
+                else:
+                    nc.scalar.activation(cv[k][:, :W], cv_ps[k][:], ACT.Copy, scale=0.0625)
+            entries = slice(c0 // 16, c1 // 16)
+            nc.scalar.activation(g3[:, k, c0:c1], cv[k][:].indirect(l_n3[:, entries]), ACT.Copy)
+            if i in N4_ON_SCALAR:
+                nc.scalar.activation(g4[:, k, c0:c1], cv[k][:].indirect(l_n4[:, entries]), ACT.Copy)
+            else:
+                nc.vector.tensor_copy(g4[:, k, c0:c1], cv[k][:].indirect(l_n4[:, entries]))
+            nc.scalar.activation(g5[:, k, c0:c1], cv[k][:].indirect(l_n5[:, entries]), ACT.Copy)
+
+        def combine(i):
+            k, c0, c1 = steps[i]
+            nc.vector.tensor_tensor(top[:, k, c0:c1], g4[:, k, c0:c1], g5[:, k, c0:c1], ALU.max)
+            nc.vector.scalar_tensor_tensor(r[:, k, c0:c1], cv_ps[k][:, c0:c1], 0.0625, g3[:, k, c0:c1], ALU.mult, ALU.add)
+            engine = nc.gpsimd if i in Y_ON_POOL else nc.vector
+            engine.tensor_tensor(y[:, k, c0:c1], r[:, k, c0:c1], top[:, k, c0:c1], ALU.subtract)
+            nc.sync.dma_start(out_rows[:, k, c0:c1], y[:, k, c0:c1])
+
+        def planes(h):
             yb = sb("yb%d" % h, [P, PACK * HALF], BF16)
-            interleave(nc.vector.tensor_copy, yb[:], y[:])
+            interleave(nc.vector.tensor_copy, yb[:], y[:, :, cols(h)])
             nc.vector.quantize_mx(y_codes[:, cols(h)].bitcast(FP8X4), y_scales[:, cols(h)], yb[:])
             nc.sync.dma_start(out_words[:, cols(h)], y_codes[:, cols(h)].bitcast(I32))
+
+        fetch(0)
+        for i in range(len(steps)):
+            if i + 1 < len(steps):
+                fetch(i + 1)
+            combine(i)
+            if steps[i][0] == PACK - 1:
+                planes(steps[i][1] // HALF)
         for q in range(4):
             queue = nc.scalar if q % 2 == 0 else nc.sync
             queue.dma_start(out_2[0, 4 * q : 4 * q + 4, :].bitcast(I32), y_scales[32 * q : 32 * q + 4, :].bitcast(I32))

@@ -16,15 +16,12 @@ P = 128
 PACK = 4
 T = 2048
 W = 512
-HALF = 256
-HL = HALF // 16
-FLOPS = 3 * 2 * 512 * 512 * 512
-GA_ON_SCALAR = ()
-SG_ON_POOL = False
-Z2_ON_SCALAR = True
-N4_ON_SCALAR = ()
-Y_ON_POOL = (0, 1, 2)
-WARM = False
+HALF = W // 2
+LANES = 16
+CV_SCALE = 0.0625
+FLOAT_MAX = 3.0e38
+CLEAR_SPLIT = 1664
+FLOPS = 3 * 2 * W * W * W
 
 
 def tile_picked_momtracktrim_none_po_kernel(
@@ -39,70 +36,30 @@ def tile_picked_momtracktrim_none_po_kernel(
             return keep.tile(shape, dtype, name=name, tag=tag or name, align_bytes=64)
 
         def load_list(name, src):
-            tile = keep.tile([P, W // 16], U16, name=name)
+            tile = keep.tile([P, W // LANES], U16, name=name)
             nc.sync.dma_start(tile[:], src)
             return tile
 
-        def half_of(lst, h):
-            return lst[:, h * HL : (h + 1) * HL]
-
-        def cols(h):
+        def half(h):
             return slice(h * HALF, (h + 1) * HALF)
 
-        xs = sb("xs", [P, T], U8)
-        nc.vector.memset(xs[:, :1664].bitcast(I32), 0)
-        nc.gpsimd.memset(xs[:, 1664:].bitcast(I32), 0)
-        if WARM:
-            warm_in = sb("warm_in", [P, 1], F32)
-            warm_out = sb("warm_out", [P, 1], F32)
-            nc.gpsimd.memset(warm_in[:], 0.0)
-            nc.scalar.activation(warm_out[:], warm_in[:], ACT.Sigmoid)
-        for q in range(4):
-            nc.sync.dma_start(xs[32 * q : 32 * q + 4, :].bitcast(I32), x_scales[0, 4 * q : 4 * q + 4, :].bitcast(I32))
-        raw = {}
+        def entries(lst, c):
+            return lst[:, c.start // LANES : c.stop // LANES]
 
         def load_weights(name, w, h):
-            raw[name, h] = sb("raw_%s%d" % (name, h), [P, PACK, HALF], F32)
-            nc.sync.dma_start(raw[name, h][:], w.rearrange("(p j) c -> p j c", j=PACK)[:, :, cols(h)])
+            raw = sb("raw_%s%d" % (name, h), [P, PACK, HALF], F32)
+            nc.sync.dma_start(raw[:], w.rearrange("(p j) c -> p j c", j=PACK)[:, :, half(h)])
+            return raw
 
-        l_offs = load_list("l_offs", offs)
-        load_weights("wa", wa, 0)
-        l_two = load_list("l_two", two)
-        load_weights("wa", wa, 1)
-        xw = sb("xw", [P, T], U32)
-        nc.sync.dma_start(xw[:].bitcast(I32), x_words[0].rearrange("p n t -> p (n t)").bitcast(I32))
-        l_n1 = load_list("l_n1", n1)
-        load_weights("wb", wb, 0)
-        load_weights("wb", wb, 1)
-        gt_sb = sb("gt_sb", [P, PACK], F32)
-        gi_sb = sb("gi_sb", [P, PACK], F32)
-        nc.sync.dma_start(gt_sb[:], gt.rearrange("(p t) o -> p (t o)", t=PACK))
-        l_n2 = load_list("l_n2", n2)
-        nc.sync.dma_start(gi_sb[:], gi.rearrange("(p t) o -> p (t o)", t=PACK))
-        l_n3 = load_list("l_n3", n3)
-        l_n5 = load_list("l_n5", n5)
-        l_n4 = load_list("l_n4", n4)
+        def load_column(name, src):
+            tile = sb(name, [P, PACK], F32)
+            nc.sync.dma_start(tile[:], src.rearrange("(p t) o -> p (t o)", t=PACK))
+            return tile
 
-        a_sb = [sb("a_sb%d" % t, [P, 2 * W], F32) for t in range(PACK)]
-        ga_sb = {t: sb("ga_sb%d" % t, [P, 2 * W], F32) for t in GA_ON_SCALAR}
-        for t in range(PACK):
-            nc.gpsimd.memset(a_sb[t][:, W:], 0.0)
-        for t in GA_ON_SCALAR:
-            nc.gpsimd.memset(ga_sb[t][:, W:], 0.0)
-
-        def dealt(tile):
-            return tile[:].rearrange("p (t m) -> p m t", t=PACK)
-
-        pick_s = {}
-        pick_w = {}
-
-        def pick_scales(name, lst):
-            pick_s[name] = sb("pick_s_" + name, [P, W], U8)
-            nc.vector.tensor_copy(dealt(pick_s[name]), xs[:].indirect(lst[:]))
-
-        def pick_words(name, lst, tag=None):
-            pick_w[name] = sb("pick_w_" + name, [P, W], U32, tag)
-            nc.vector.tensor_copy(dealt(pick_w[name]), xw[:].indirect(lst[:]))
+        def pick(name, table, lst, dtype):
+            picked = sb(name, [P, W], dtype)
+            nc.vector.tensor_copy(picked[:].rearrange("p (t m) -> p m t", t=PACK), table[:].indirect(lst[:]))
+            return picked
 
         def interleave(copy, dst, src):
             copy(
@@ -110,142 +67,152 @@ def tile_picked_momtracktrim_none_po_kernel(
                 src.rearrange("p t (c i) -> p c t i", i=4),
             )
 
-        w_codes = {}
-        w_scales = {}
-
-        def weights(name, engines):
-            rounded = []
+        def quantise_weights(name, copy, raw):
+            rounded = sb("round_" + name, [P, PACK * W], BF16)
             for h in range(2):
-                r = sb("round_%s%d" % (name, h), [P, PACK * HALF], BF16)
-                interleave(engines[h], r[:], raw[name, h][:])
-                rounded.append(r)
-            return rounded
+                interleave(copy, rounded[:, h * PACK * HALF : (h + 1) * PACK * HALF], raw[h][:])
+            mx = (sb(name + "_codes", [P, W], U32), sb(name + "_scales", [P, W], U8))
+            quantise(*mx, slice(0, W), rounded[:])
+            return mx
 
-        def quantise_weights(name, rounded):
-            w_codes[name] = sb("codes_" + name, [P, W], U32)
-            w_scales[name] = sb("scales_" + name, [P, W], U8, "xs" if name == "wa" else None)
-            for h in range(2):
-                nc.vector.quantize_mx(w_codes[name][:, cols(h)].bitcast(FP8X4), w_scales[name][:, cols(h)], rounded[h][:])
+        def quantise(codes, scales, columns, values):
+            nc.vector.quantize_mx(codes[:, columns].bitcast(FP8X4), scales[:, columns], values)
 
-        def product(bank, lc, ls, t, rc, rs):
+        def product(name, bank, t, rows, columns, c=slice(0, W)):
+            tile = psum.tile([P, c.stop - c.start], F32, name="%s%d" % (name, bank), tag="bank%d" % bank)
             m = slice(t * P, (t + 1) * P)
             nc.tensor.matmul_mx(
-                bank[:], lhsT=lc[:, m].bitcast(FP8X4), lhsT_scale=ls[:, m], rhs=rc[:].bitcast(FP8X4), rhs_scale=rs[:],
-                start=True, stop=True,
+                tile[:],
+                lhsT=rows[0][:, m].bitcast(FP8X4),
+                lhsT_scale=rows[1][:, m],
+                rhs=columns[0][:, c].bitcast(FP8X4),
+                rhs_scale=columns[1][:, c],
+                start=True,
+                stop=True,
             )
+            return tile
 
-        pick_scales("wa", l_offs)
-        pick_scales("wb", l_two)
-        quantise_weights("wa", weights("wa", (nc.scalar.copy, nc.scalar.copy)))
-        pick_words("wa", l_offs)
-        a_ps = [psum.tile([P, W], F32, name="a_ps%d" % t, tag="bank%d" % t) for t in range(PACK)]
+        xs = sb("xs", [P, T], U8)
+        nc.vector.memset(xs[:, :CLEAR_SPLIT].bitcast(I32), 0)
+        nc.gpsimd.memset(xs[:, CLEAR_SPLIT:].bitcast(I32), 0)
+        for q in range(4):
+            nc.sync.dma_start(xs[32 * q : 32 * q + 4, :].bitcast(I32), x_scales[0, 4 * q : 4 * q + 4, :].bitcast(I32))
+        l_offs = load_list("l_offs", offs)
+        raw_wa = [load_weights("wa", wa, 0)]
+        l_two = load_list("l_two", two)
+        raw_wa.append(load_weights("wa", wa, 1))
+        xw = sb("xw", [P, T], U32)
+        nc.sync.dma_start(xw[:].bitcast(I32), x_words[0].rearrange("p n t -> p (n t)").bitcast(I32))
+        gt_sb = load_column("gt_sb", gt)
+        l_n1 = load_list("l_n1", n1)
+        raw_wb = [load_weights("wb", wb, h) for h in range(2)]
+        l_n2 = load_list("l_n2", n2)
+        gi_sb = load_column("gi_sb", gi)
+        l_n3 = load_list("l_n3", n3)
+        l_n5 = load_list("l_n5", n5)
+        l_n4 = load_list("l_n4", n4)
+
+        window = [sb("window%d" % t, [P, 2 * W], F32) for t in range(PACK)]
         for t in range(PACK):
-            product(a_ps[t], pick_w["wa"], pick_s["wa"], t, w_codes["wa"], w_scales["wa"])
-        pick_words("wb", l_two)
-        quantise_weights("wb", weights("wb", (nc.vector.tensor_copy, nc.vector.tensor_copy)))
-        b_ps = [psum.tile([P, W], F32, name="b_ps%d" % j, tag="bank%d" % (4 + j)) for j in range(PACK)]
-        for j in range(PACK):
-            product(b_ps[j], pick_w["wb"], pick_s["wb"], j, w_codes["wb"], w_scales["wb"])
+            nc.gpsimd.memset(window[t][:, W:], 0.0)
 
-        zb = sb("zb", [P, PACK * W], BF16)
-        z2p = sb("z2p", [P, PACK, W], BF16)
+        xa_scales = pick("xa_scales", xs, l_offs, U8)
+        xb_scales = pick("xb_scales", xs, l_two, U8)
+        wa_mx = quantise_weights("wa", nc.scalar.copy, raw_wa)
+        xa_mx = (pick("xa_words", xw, l_offs, U32), xa_scales)
+        a_ps = [product("a_ps", t, t, xa_mx, wa_mx) for t in range(PACK)]
+        xb_mx = (pick("xb_words", xw, l_two, U32), xb_scales)
+
+        gt_zero = sb("gt_zero", [P, PACK], F32)
+        gt_safe = sb("gt_safe", [P, PACK], F32)
+        gt_recip = sb("gt_recip", [P, PACK], F32)
+        gt_inv = sb("gt_inv", [P, PACK], F32)
+        nc.gpsimd.tensor_scalar(gt_zero[:], gt_sb[:], 0.0, None, ALU.is_equal)
+        nc.gpsimd.tensor_tensor(gt_safe[:], gt_sb[:], gt_zero[:], ALU.add)
+        nc.vector.reciprocal(gt_recip[:], gt_safe[:])
+        nc.gpsimd.tensor_scalar(gt_inv[:], gt_recip[:], FLOAT_MAX, -FLOAT_MAX, ALU.min, ALU.max)
+
+        wb_mx = quantise_weights("wb", nc.vector.tensor_copy, raw_wb)
+        b_ps = [product("b_ps", PACK + t, t, xb_mx, wb_mx) for t in range(PACK)]
+
         s = sb("s", [P, PACK, W], F32)
-        sg = sb("sg", [P, PACK, W], F32, "round_wb1")
-        v = sb("v", [P, PACK, W], F32)
-        u = sb("u", [P, PACK, W], F32)
-
-        def gate(t):
-            gt_col = gt_sb[:, t : t + 1]
-            nc.scalar.copy(a_sb[t][:, :W], a_ps[t][:])
-            nc.scalar.activation(s[:, t, :], a_sb[t][:].indirect(l_n1[:]), ACT.Sigmoid)
-            if t in ():
-                nc.gpsimd.tensor_scalar(sg[:, t, :], s[:, t, :], gt_col, 0.0, ALU.mult, ALU.add)
-            elif t in (3,):
-                nc.scalar.activation(sg[:, t, :], s[:, t, :], ACT.Copy, scale=gt_col)
-            else:
-                nc.vector.tensor_scalar(sg[:, t, :], s[:, t, :], gt_col, None, ALU.mult)
-
-        gate(0)
+        vu = sb("vu", [P, 2 * PACK, W], F32, "round_wb")
+        v = vu[:, :PACK, :]
+        u = vu[:, PACK:, :]
         for t in range(PACK):
-            nc.vector.tensor_tensor(v[:, t, :], a_sb[t][:].indirect(l_n2[:]), sg[:, t, :], ALU.mult)
-            if t + 1 < PACK:
-                gate(t + 1)
-            nc.vector.scalar_tensor_tensor(
-                u[:, t, :], sg[:, t, :], gt_sb[:, t : t + 1], a_ps[t][:], ALU.subtract, ALU.mult
-            )
+            ga = window[t]
+            nc.scalar.activation(ga[:, :W], a_ps[t][:], ACT.Copy, scale=gt_sb[:, t : t + 1])
+            for c in (half(0), half(1)) if t == 0 else (slice(0, W),):
+                nc.scalar.activation(
+                    s[:, t, c], ga[:].indirect(entries(l_n1, c)), ACT.Sigmoid, scale=gt_inv[:, t : t + 1]
+                )
+                nc.vector.tensor_tensor(v[:, t, c], ga[:].indirect(entries(l_n2, c)), s[:, t, c], ALU.mult)
+            nc.vector.scalar_tensor_tensor(u[:, t, :], s[:, t, :], -1.0, ga[:, :W], ALU.add, ALU.mult)
+        z2_rows = sb("z2_rows", [P, PACK, W], BF16)
         for t in range(PACK):
-            nc.scalar.activation(z2p[:, t, :], b_ps[t][:], ACT.Copy, scale=gi_sb[:, t : t + 1])
-        z2b = sb("z2b", [P, PACK * W], BF16)
-        z2_scales = sb("z2_scales", [P, W], U8)
-        if Z2_ON_SCALAR:
-            interleave(nc.scalar.copy, z2b[:], z2p[:])
+            nc.scalar.activation(z2_rows[:, t, :], b_ps[t][:], ACT.Copy, scale=gi_sb[:, t : t + 1])
+        z2 = sb("z2", [P, PACK * W], BF16)
+        interleave(nc.scalar.copy, z2[:], z2_rows[:])
+        z = sb("z", [P, PACK * W], BF16)
         nc.vector.tensor_tensor(
-            zb[:].rearrange("p (k m t) -> p m t k", k=PACK, t=PACK),
-            v[:].rearrange("p t (m k) -> p m t k", k=PACK),
-            u[:].rearrange("p t (m k) -> p m t k", k=PACK),
+            z[:].rearrange("p (k m t) -> p m t k", k=PACK, t=PACK),
+            v.rearrange("p t (m k) -> p m t k", k=PACK),
+            u.rearrange("p t (m k) -> p m t k", k=PACK),
             ALU.subtract,
         )
-        if not Z2_ON_SCALAR:
-            interleave(nc.vector.tensor_copy, z2b[:], z2p[:])
-        z_codes = sb("z_codes", [P, W], U32)
-        z_scales = sb("z_scales", [P, W], U8)
-        cv_ps = [psum.tile([P, W], F32, name="cv_ps%d" % k, tag="bank%d" % k) for k in range(PACK)]
-        z2_codes = sb("z2_codes", [P, W], U32, "v")
-        nc.vector.quantize_mx(z2_codes[:].bitcast(FP8X4), z2_scales[:], z2b[:])
+        z2_mx = (sb("z2_codes", [P, W], U32, "round_wb"), sb("z2_scales", [P, W], U8))
+        quantise(*z2_mx, slice(0, W), z2[:])
+        z_mx = (sb("z_codes", [P, W], U32), sb("z_scales", [P, W], U8))
+        cv_ps = {}
         for k in range(PACK):
-            m = slice(k * P, (k + 1) * P)
-            nc.vector.quantize_mx(z_codes[:, m].bitcast(FP8X4), z_scales[:, m], zb[:, k * W : (k + 1) * W])
-            product(cv_ps[k], z_codes, z_scales, k, z2_codes, z2_scales)
+            quantise(*z_mx, slice(k * P, (k + 1) * P), z[:, k * W : (k + 1) * W])
+            if k == 0:
+                cv_first = [product("cv_ps", PACK + h, k, z_mx, z2_mx, half(h)) for h in range(2)]
+            else:
+                cv_ps[k] = product("cv_ps", k, k, z_mx, z2_mx)
 
-        cv = a_sb
-        y_codes = sb("y_codes", [P, W], U32)
-        y_scales = sb("y_scales", [P, W], U8)
         out_rows = out_0.rearrange("(p k) n -> p k n", k=PACK)
         out_words = out_1[0].rearrange("p n t -> p (n t)").bitcast(I32)
         g3 = sb("g3", [P, PACK, W], F32)
         g4 = sb("g4", [P, PACK, W], F32)
         g5 = sb("g5", [P, PACK, W], F32)
         top = sb("top", [P, PACK, W], F32)
-        r = sb("r", [P, PACK, W], F32)
+        kept = sb("kept", [P, PACK, W], F32)
         y = sb("y", [P, PACK, W], F32)
-        steps = [(0, 0, W), (1, 0, W), (2, 0, W), (3, 0, HALF), (3, HALF, W)]
+        pieces = [(k, slice(0, W)) for k in range(PACK - 1)] + [(PACK - 1, half(h)) for h in range(2)]
 
-        def fetch(i):
-            k, c0, c1 = steps[i]
-            if c0 == 0:
-                if k in (1, 2):
-                    nc.vector.tensor_scalar(cv[k][:, :W], cv_ps[k][:], 0.0625, None, ALU.mult)
+        def fetch(k, c):
+            cv = window[k]
+            if c.start == 0:
+                if k == 0:
+                    nc.scalar.activation(cv[:, half(0)], cv_first[0][:], ACT.Copy, scale=CV_SCALE)
+                    nc.vector.tensor_scalar(cv[:, half(1)], cv_first[1][:], CV_SCALE, None, ALU.mult)
+                elif k == 1:
+                    nc.vector.tensor_scalar(cv[:, :W], cv_ps[k][:], CV_SCALE, None, ALU.mult)
                 else:
-                    nc.scalar.activation(cv[k][:, :W], cv_ps[k][:], ACT.Copy, scale=0.0625)
-            entries = slice(c0 // 16, c1 // 16)
-            nc.scalar.activation(g3[:, k, c0:c1], cv[k][:].indirect(l_n3[:, entries]), ACT.Copy)
-            if i in N4_ON_SCALAR:
-                nc.scalar.activation(g4[:, k, c0:c1], cv[k][:].indirect(l_n4[:, entries]), ACT.Copy)
-            else:
-                nc.vector.tensor_copy(g4[:, k, c0:c1], cv[k][:].indirect(l_n4[:, entries]))
-            nc.scalar.activation(g5[:, k, c0:c1], cv[k][:].indirect(l_n5[:, entries]), ACT.Copy)
+                    nc.scalar.activation(cv[:, :W], cv_ps[k][:], ACT.Copy, scale=CV_SCALE)
+            nc.scalar.activation(g3[:, k, c], cv[:].indirect(entries(l_n3, c)), ACT.Copy)
+            nc.vector.tensor_copy(g4[:, k, c], cv[:].indirect(entries(l_n4, c)))
+            nc.scalar.activation(g5[:, k, c], cv[:].indirect(entries(l_n5, c)), ACT.Copy)
 
-        def combine(i):
-            k, c0, c1 = steps[i]
-            nc.vector.tensor_tensor(top[:, k, c0:c1], g4[:, k, c0:c1], g5[:, k, c0:c1], ALU.max)
-            nc.vector.scalar_tensor_tensor(r[:, k, c0:c1], cv_ps[k][:, c0:c1], 0.0625, g3[:, k, c0:c1], ALU.mult, ALU.add)
-            engine = nc.gpsimd if i in Y_ON_POOL else nc.vector
-            engine.tensor_tensor(y[:, k, c0:c1], r[:, k, c0:c1], top[:, k, c0:c1], ALU.subtract)
-            nc.sync.dma_start(out_rows[:, k, c0:c1], y[:, k, c0:c1])
+        def combine(k, c):
+            nc.vector.tensor_tensor(top[:, k, c], g4[:, k, c], g5[:, k, c], ALU.max)
+            nc.vector.tensor_tensor(kept[:, k, c], window[k][:, c], g3[:, k, c], ALU.add)
+            nc.vector.tensor_tensor(y[:, k, c], kept[:, k, c], top[:, k, c], ALU.subtract)
+            nc.sync.dma_start(out_rows[:, k, c], y[:, k, c])
 
-        def planes(h):
-            yb = sb("yb%d" % h, [P, PACK * HALF], BF16)
-            interleave(nc.vector.tensor_copy, yb[:], y[:, :, cols(h)])
-            nc.vector.quantize_mx(y_codes[:, cols(h)].bitcast(FP8X4), y_scales[:, cols(h)], yb[:])
-            nc.sync.dma_start(out_words[:, cols(h)], y_codes[:, cols(h)].bitcast(I32))
-
-        fetch(0)
-        for i in range(len(steps)):
-            if i + 1 < len(steps):
-                fetch(i + 1)
-            combine(i)
-            if steps[i][0] == PACK - 1:
-                planes(steps[i][1] // HALF)
+        fetch(*pieces[0])
+        for i, piece in enumerate(pieces):
+            if i + 1 < len(pieces):
+                fetch(*pieces[i + 1])
+            combine(*piece)
+        y_mx = (sb("y_codes", [P, W], U32), sb("y_scales", [P, W], U8))
+        y_rounded = [sb("y_rounded%d" % h, [P, PACK * HALF], BF16) for h in range(2)]
+        interleave(nc.scalar.copy, y_rounded[0][:], y[:, :, half(0)])
+        interleave(nc.vector.tensor_copy, y_rounded[1][:], y[:, :, half(1)])
+        for h in range(2):
+            quantise(*y_mx, half(h), y_rounded[h][:])
+            nc.sync.dma_start(out_words[:, half(h)], y_mx[0][:, half(h)].bitcast(I32))
         for q in range(4):
             queue = nc.scalar if q % 2 == 0 else nc.sync
-            queue.dma_start(out_2[0, 4 * q : 4 * q + 4, :].bitcast(I32), y_scales[32 * q : 32 * q + 4, :].bitcast(I32))
+            queue.dma_start(out_2[0, 4 * q : 4 * q + 4, :].bitcast(I32), y_mx[1][32 * q : 32 * q + 4, :].bitcast(I32))

@@ -1,6 +1,7 @@
 from contextlib import ExitStack
 
 import concourse.mybir as mybir
+from concourse.masks import make_identity
 
 F32 = mybir.dt.float32
 BF16 = mybir.dt.bfloat16
@@ -17,6 +18,7 @@ PACK = 4
 T = 2048
 W = 512
 HALF = W // 2
+RUN = 8
 LANES = 16
 CV_SCALE = 0.0625
 FLOAT_MAX = 3.0e38
@@ -51,14 +53,25 @@ def tile_picked_momtracktrim_none_po_kernel(
             nc.sync.dma_start(raw[:], w.rearrange("(p j) c -> p j c", j=PACK)[:, :, half(h)])
             return raw
 
-        def load_column(name, src):
-            tile = sb(name, [P, PACK], F32)
-            nc.sync.dma_start(tile[:], src.rearrange("(p t) o -> p (t o)", t=PACK))
-            return tile
+        def load_place_weights(name, src):
+            rows = sb(name, [P, P], F32)
+            nc.vector.memset(rows[:], 0.0)
+            nc.gpsimd.dma_start(
+                rows[:PACK, :].rearrange("t (q r) -> t q r", r=RUN),
+                src.rearrange("(q t r) o -> t q (r o)", t=PACK, r=RUN),
+            )
+            return rows
+
+        def turn(name, rows, bank, tag=None):
+            turned = psum.tile([P, P], F32, name=name + "_ps", tag="bank%d" % bank)
+            nc.tensor.transpose(turned[:], rows[:], identity[:])
+            columns = sb(name, [P, PACK], F32, tag)
+            nc.scalar.copy(columns[:], turned[:, :PACK])
+            return columns
 
         def pick(name, table, lst, dtype):
             picked = sb(name, [P, W], dtype)
-            nc.vector.tensor_copy(picked[:].rearrange("p (t m) -> p m t", t=PACK), table[:].indirect(lst[:]))
+            nc.vector.tensor_copy(picked[:].rearrange("p (t q r) -> p q t r", t=PACK, r=RUN), table[:].indirect(lst[:]))
             return picked
 
         def interleave(copy, dst, src):
@@ -103,29 +116,32 @@ def tile_picked_momtracktrim_none_po_kernel(
         raw_wa.append(load_weights("wa", wa, 1))
         xw = sb("xw", [P, T], U32)
         nc.sync.dma_start(xw[:].bitcast(I32), x_words[0].rearrange("p n t -> p (n t)").bitcast(I32))
-        gt_sb = load_column("gt_sb", gt)
         l_n1 = load_list("l_n1", n1)
         raw_wb = [load_weights("wb", wb, h) for h in range(2)]
         l_n2 = load_list("l_n2", n2)
-        gi_sb = load_column("gi_sb", gi)
         l_n3 = load_list("l_n3", n3)
         l_n5 = load_list("l_n5", n5)
         l_n4 = load_list("l_n4", n4)
 
+        gt_rows = load_place_weights("gt_rows", gt)
+        gi_rows = load_place_weights("gi_rows", gi)
+        identity = sb("identity", [P, P], F32)
+        make_identity(nc, identity[:])
         window = [sb("window%d" % t, [P, 2 * W], F32) for t in range(PACK)]
         for t in range(PACK):
-            nc.gpsimd.memset(window[t][:, W:], 0.0)
+            nc.vector.memset(window[t][:, W:], 0.0)
 
         xa_scales = pick("xa_scales", xs, l_offs, U8)
         xb_scales = pick("xb_scales", xs, l_two, U8)
         wa_mx = quantise_weights("wa", nc.scalar.copy, raw_wa)
+        gt_sb = turn("gt_sb", gt_rows, 7, "raw_wa1")
         xa_mx = (pick("xa_words", xw, l_offs, U32), xa_scales)
         a_ps = [product("a_ps", t, t, xa_mx, wa_mx) for t in range(PACK)]
         xb_mx = (pick("xb_words", xw, l_two, U32), xb_scales)
 
         gt_zero = sb("gt_zero", [P, PACK], F32)
         gt_safe = sb("gt_safe", [P, PACK], F32)
-        gt_recip = sb("gt_recip", [P, PACK], F32)
+        gt_recip = sb("gt_recip", [P, PACK], F32, "xw")
         gt_inv = sb("gt_inv", [P, PACK], F32)
         nc.gpsimd.tensor_scalar(gt_zero[:], gt_sb[:], 0.0, None, ALU.is_equal)
         nc.gpsimd.tensor_tensor(gt_safe[:], gt_sb[:], gt_zero[:], ALU.add)
@@ -148,6 +164,7 @@ def tile_picked_momtracktrim_none_po_kernel(
                 )
                 nc.vector.tensor_tensor(v[:, t, c], ga[:].indirect(entries(l_n2, c)), s[:, t, c], ALU.mult)
             nc.vector.scalar_tensor_tensor(u[:, t, :], s[:, t, :], -1.0, ga[:, :W], ALU.add, ALU.mult)
+        gi_sb = turn("gi_sb", gi_rows, 0)
         z2_rows = sb("z2_rows", [P, PACK, W], BF16)
         for t in range(PACK):
             nc.scalar.activation(z2_rows[:, t, :], b_ps[t][:], ACT.Copy, scale=gi_sb[:, t : t + 1])

@@ -108,6 +108,10 @@ def tile_picked_momtracktrim_none_po_kernel(
         xs = sb("xs", [P, T], U8)
         nc.vector.memset(xs[:, :CLEAR_SPLIT].bitcast(I32), 0)
         nc.gpsimd.memset(xs[:, CLEAR_SPLIT:].bitcast(I32), 0)
+        warm_in = sb("warm_in", [P, 1], F32)
+        warm_out = sb("warm_out", [P, 1], F32)
+        nc.gpsimd.memset(warm_in[:], 0.0)
+        nc.scalar.activation(warm_out[:], warm_in[:], ACT.Sigmoid)
         for q in range(4):
             nc.sync.dma_start(xs[32 * q : 32 * q + 4, :].bitcast(I32), x_scales[0, 4 * q : 4 * q + 4, :].bitcast(I32))
         l_offs = load_list("l_offs", offs)

from contextlib import ExitStack

import concourse.mybir as mybir
from concourse.masks import make_identity

F32 = mybir.dt.float32
BF16 = mybir.dt.bfloat16
I32 = mybir.dt.int32
U32 = mybir.dt.uint32
U16 = mybir.dt.uint16
U8 = mybir.dt.uint8
FP8X4 = mybir.dt.float8_e4m3fn_x4
ALU = mybir.AluOpType
ACT = mybir.ActivationFunctionType

P = 128
PACK = 4
T = 2048
W = 512
HALF = W // 2
RUN = 8
LANES = 16
CV_SCALE = 0.0625
FLOAT_MAX = 3.0e38
CLEAR_SPLIT = 1664
FLOPS = 3 * 2 * W * W * W


def tile_picked_momtracktrim_none_po_kernel(
    tc, x_words, x_scales, wa, wb, gt, gi, offs, two, n1, n2, n3, n4, n5, out_0, out_1, out_2
):
    nc = tc.nc
    with ExitStack() as ctx:
        keep = ctx.enter_context(tc.tile_pool(name="keep", bufs=1))
        psum = ctx.enter_context(tc.psum_pool(name="psum", bufs=1))

        def sb(name, shape, dtype, tag=None):
            return keep.tile(shape, dtype, name=name, tag=tag or name, align_bytes=64)

        def load_list(name, src):
            tile = keep.tile([P, W // LANES], U16, name=name)
            nc.sync.dma_start(tile[:], src)
            return tile

        def half(h):
            return slice(h * HALF, (h + 1) * HALF)

        def entries(lst, c):
            return lst[:, c.start // LANES : c.stop // LANES]

        def load_weights(name, w, h):
            raw = sb("raw_%s%d" % (name, h), [P, PACK, HALF], F32)
            nc.sync.dma_start(raw[:], w.rearrange("(p j) c -> p j c", j=PACK)[:, :, half(h)])
            return raw

        def load_place_weights(name, src):
            rows = sb(name, [P, P], F32)
            nc.vector.memset(rows[:], 0.0)
            nc.gpsimd.dma_start(
                rows[:PACK, :].rearrange("t (q r) -> t q r", r=RUN),
                src.rearrange("(q t r) o -> t q (r o)", t=PACK, r=RUN),
            )
            return rows

        def turn(name, rows, bank, tag=None):
            turned = psum.tile([P, P], F32, name=name + "_ps", tag="bank%d" % bank)
            nc.tensor.transpose(turned[:], rows[:], identity[:])
            columns = sb(name, [P, PACK], F32, tag)
            nc.scalar.copy(columns[:], turned[:, :PACK])
            return columns

        def pick(name, table, lst, dtype):
            picked = sb(name, [P, W], dtype)
            nc.vector.tensor_copy(picked[:].rearrange("p (t q r) -> p q t r", t=PACK, r=RUN), table[:].indirect(lst[:]))
            return picked

        def interleave(copy, dst, src):
            copy(
                dst.rearrange("p (c i t) -> p c t i", i=4, t=PACK),
                src.rearrange("p t (c i) -> p c t i", i=4),
            )

        def quantise_weights(name, copy, raw):
            rounded = sb("round_" + name, [P, PACK * W], BF16)
            for h in range(2):
                interleave(copy, rounded[:, h * PACK * HALF : (h + 1) * PACK * HALF], raw[h][:])
            mx = (sb(name + "_codes", [P, W], U32), sb(name + "_scales", [P, W], U8))
            quantise(*mx, slice(0, W), rounded[:])
            return mx

        def quantise(codes, scales, columns, values):
            nc.vector.quantize_mx(codes[:, columns].bitcast(FP8X4), scales[:, columns], values)

        def product(name, bank, t, rows, columns, c=slice(0, W)):
            tile = psum.tile([P, c.stop - c.start], F32, name="%s%d" % (name, bank), tag="bank%d" % bank)
            m = slice(t * P, (t + 1) * P)
            nc.tensor.matmul_mx(
                tile[:],
                lhsT=rows[0][:, m].bitcast(FP8X4),
                lhsT_scale=rows[1][:, m],
                rhs=columns[0][:, c].bitcast(FP8X4),
                rhs_scale=columns[1][:, c],
                start=True,
                stop=True,
            )
            return tile

        xs = sb("xs", [P, T], U8)
        nc.vector.memset(xs[:, :CLEAR_SPLIT].bitcast(I32), 0)
        nc.gpsimd.memset(xs[:, CLEAR_SPLIT:].bitcast(I32), 0)
        warm_in = sb("warm_in", [P, 1], F32)
        warm_out = sb("warm_out", [P, 1], F32)
        nc.gpsimd.memset(warm_in[:], 0.0)
        nc.scalar.activation(warm_out[:], warm_in[:], ACT.Sigmoid)
        for q in range(4):
            nc.sync.dma_start(xs[32 * q : 32 * q + 4, :].bitcast(I32), x_scales[0, 4 * q : 4 * q + 4, :].bitcast(I32))
        l_offs = load_list("l_offs", offs)
        raw_wa = [load_weights("wa", wa, 0)]
        l_two = load_list("l_two", two)
        raw_wa.append(load_weights("wa", wa, 1))
        xw = sb("xw", [P, T], U32)
        nc.sync.dma_start(xw[:].bitcast(I32), x_words[0].rearrange("p n t -> p (n t)").bitcast(I32))
        l_n1 = load_list("l_n1", n1)
        raw_wb = [load_weights("wb", wb, h) for h in range(2)]
        l_n2 = load_list("l_n2", n2)
        l_n3 = load_list("l_n3", n3)
        l_n5 = load_list("l_n5", n5)
        l_n4 = load_list("l_n4", n4)

        gt_rows = load_place_weights("gt_rows", gt)
        gi_rows = load_place_weights("gi_rows", gi)
        identity = sb("identity", [P, P], F32)
        make_identity(nc, identity[:])
        window = [sb("window%d" % t, [P, 2 * W], F32) for t in range(PACK)]
        for t in range(PACK):
            nc.vector.memset(window[t][:, W:], 0.0)

        xa_scales = pick("xa_scales", xs, l_offs, U8)
        xb_scales = pick("xb_scales", xs, l_two, U8)
        wa_mx = quantise_weights("wa", nc.scalar.copy, raw_wa)
        gt_sb = turn("gt_sb", gt_rows, 7, "raw_wa1")
        xa_mx = (pick("xa_words", xw, l_offs, U32), xa_scales)
        a_ps = [product("a_ps", t, t, xa_mx, wa_mx) for t in range(PACK)]
        xb_mx = (pick("xb_words", xw, l_two, U32), xb_scales)

        gt_zero = sb("gt_zero", [P, PACK], F32)
        gt_safe = sb("gt_safe", [P, PACK], F32)
        gt_recip = sb("gt_recip", [P, PACK], F32, "xw")
        gt_inv = sb("gt_inv", [P, PACK], F32)
        nc.gpsimd.tensor_scalar(gt_zero[:], gt_sb[:], 0.0, None, ALU.is_equal)
        nc.gpsimd.tensor_tensor(gt_safe[:], gt_sb[:], gt_zero[:], ALU.add)
        nc.vector.reciprocal(gt_recip[:], gt_safe[:])
        nc.gpsimd.tensor_scalar(gt_inv[:], gt_recip[:], FLOAT_MAX, -FLOAT_MAX, ALU.min, ALU.max)

        wb_mx = quantise_weights("wb", nc.vector.tensor_copy, raw_wb)
        b_ps = [product("b_ps", PACK + t, t, xb_mx, wb_mx) for t in range(PACK)]

        s = sb("s", [P, PACK, W], F32)
        vu = sb("vu", [P, 2 * PACK, W], F32, "round_wb")
        v = vu[:, :PACK, :]
        u = vu[:, PACK:, :]
        for t in range(PACK):
            ga = window[t]
            nc.scalar.activation(ga[:, :W], a_ps[t][:], ACT.Copy, scale=gt_sb[:, t : t + 1])
            for c in (half(0), half(1)) if t == 0 else (slice(0, W),):
                nc.scalar.activation(
                    s[:, t, c], ga[:].indirect(entries(l_n1, c)), ACT.Sigmoid, scale=gt_inv[:, t : t + 1]
                )
                nc.vector.tensor_tensor(v[:, t, c], ga[:].indirect(entries(l_n2, c)), s[:, t, c], ALU.mult)
            nc.vector.scalar_tensor_tensor(u[:, t, :], s[:, t, :], -1.0, ga[:, :W], ALU.add, ALU.mult)
        gi_sb = turn("gi_sb", gi_rows, 0)
        z2_rows = sb("z2_rows", [P, PACK, W], BF16)
        for t in range(PACK):
            nc.scalar.activation(z2_rows[:, t, :], b_ps[t][:], ACT.Copy, scale=gi_sb[:, t : t + 1])
        z2 = sb("z2", [P, PACK * W], BF16)
        interleave(nc.scalar.copy, z2[:], z2_rows[:])
        z = sb("z", [P, PACK * W], BF16)
        nc.vector.tensor_tensor(
            z[:].rearrange("p (k m t) -> p m t k", k=PACK, t=PACK),
            v.rearrange("p t (m k) -> p m t k", k=PACK),
            u.rearrange("p t (m k) -> p m t k", k=PACK),
            ALU.subtract,
        )
        z2_mx = (sb("z2_codes", [P, W], U32, "round_wb"), sb("z2_scales", [P, W], U8))
        quantise(*z2_mx, slice(0, W), z2[:])
        z_mx = (sb("z_codes", [P, W], U32), sb("z_scales", [P, W], U8))
        cv_ps = {}
        for k in range(PACK):
            quantise(*z_mx, slice(k * P, (k + 1) * P), z[:, k * W : (k + 1) * W])
            if k == 0:
                cv_first = [product("cv_ps", PACK + h, k, z_mx, z2_mx, half(h)) for h in range(2)]
            else:
                cv_ps[k] = product("cv_ps", k, k, z_mx, z2_mx)

        out_rows = out_0.rearrange("(p k) n -> p k n", k=PACK)
        out_words = out_1[0].rearrange("p n t -> p (n t)").bitcast(I32)
        g3 = sb("g3", [P, PACK, W], F32)
        g4 = sb("g4", [P, PACK, W], F32)
        g5 = sb("g5", [P, PACK, W], F32)
        top = sb("top", [P, PACK, W], F32)
        kept = sb("kept", [P, PACK, W], F32)
        y = sb("y", [P, PACK, W], F32)
        pieces = [(k, slice(0, W)) for k in range(PACK - 1)] + [(PACK - 1, half(h)) for h in range(2)]

        def fetch(k, c):
            cv = window[k]
            if c.start == 0:
                if k == 0:
                    nc.scalar.activation(cv[:, half(0)], cv_first[0][:], ACT.Copy, scale=CV_SCALE)
                    nc.vector.tensor_scalar(cv[:, half(1)], cv_first[1][:], CV_SCALE, None, ALU.mult)
                elif k == 1:
                    nc.vector.tensor_scalar(cv[:, :W], cv_ps[k][:], CV_SCALE, None, ALU.mult)
                else:
                    nc.scalar.activation(cv[:, :W], cv_ps[k][:], ACT.Copy, scale=CV_SCALE)
            nc.scalar.activation(g3[:, k, c], cv[:].indirect(entries(l_n3, c)), ACT.Copy)
            nc.vector.tensor_copy(g4[:, k, c], cv[:].indirect(entries(l_n4, c)))
            nc.scalar.activation(g5[:, k, c], cv[:].indirect(entries(l_n5, c)), ACT.Copy)

        def combine(k, c):
            nc.vector.tensor_tensor(top[:, k, c], g4[:, k, c], g5[:, k, c], ALU.max)
            nc.vector.tensor_tensor(kept[:, k, c], window[k][:, c], g3[:, k, c], ALU.add)
            nc.vector.tensor_tensor(y[:, k, c], kept[:, k, c], top[:, k, c], ALU.subtract)
            nc.sync.dma_start(out_rows[:, k, c], y[:, k, c])

        fetch(*pieces[0])
        for i, piece in enumerate(pieces):
            if i + 1 < len(pieces):
                fetch(*pieces[i + 1])
            combine(*piece)
        y_mx = (sb("y_codes", [P, W], U32), sb("y_scales", [P, W], U8))
        y_rounded = [sb("y_rounded%d" % h, [P, PACK * HALF], BF16) for h in range(2)]
        interleave(nc.scalar.copy, y_rounded[0][:], y[:, :, half(0)])
        interleave(nc.vector.tensor_copy, y_rounded[1][:], y[:, :, half(1)])
        for h in range(2):
            quantise(*y_mx, half(h), y_rounded[h][:])
            nc.sync.dma_start(out_words[:, half(h)], y_mx[0][:, half(h)].bitcast(I32))
        for q in range(4):
            queue = nc.scalar if q % 2 == 0 else nc.sync
            queue.dma_start(out_2[0, 4 * q : 4 * q + 4, :].bitcast(I32), y_mx[1][32 * q : 32 * q + 4, :].bitcast(I32))
